import numpy as np
import ml_dtypes


def mxq(x, axis, fmt="e4m3"):
    dtype, down = {"e4m3": (ml_dtypes.float8_e4m3fn, 7), "e5m2": (ml_dtypes.float8_e5m2, 14)}[fmt]
    v = np.moveaxis(np.asarray(x, np.float32).astype(ml_dtypes.bfloat16).astype(np.float64), axis, -1)
    blocks = v.reshape(v.shape[:-1] + (-1, 32))
    amax = np.abs(blocks).max(-1, keepdims=True)
    byte = np.maximum(np.where(amax > 0, np.frexp(amax)[1] - 1 + 127, 0) - down, 1)
    scale = np.exp2(byte - 127.0)
    codes = (blocks / scale).astype(np.float32).astype(dtype).astype(np.float64)
    return np.moveaxis((codes * scale).reshape(v.shape), -1, axis)


WIDE = False


def mx_kscale(k):
    if not WIDE:
        return np.ones(k)
    levels = np.array([10, -10, 5, -5, 0])
    if k % 512:
        return np.exp2(np.random.permutation(np.resize(levels, k // 32))).repeat(32)
    a = np.empty((k // 512, 16))
    for p in range(k // 512):
        a[p, :8] = np.random.permutation(np.resize(levels, 8))
        for g in range(8):
            far = levels[np.abs(levels - a[p, g]) >= 10]
            a[p, g + 8] = far[np.random.randint(len(far))]
    return np.exp2(a.ravel()).repeat(32)


def f64(x):
    return np.asarray(x).astype(np.float64)


def striped(idx):
    return np.tile(np.asarray(idx).reshape(-1, 16).T, (8, 1)).astype(np.uint16)


def unstriped(offs):
    return offs[:16].T.reshape(-1).astype(np.int64)


def striped8(idx):
    return np.asarray(idx).reshape(8, -1, 16).transpose(0, 2, 1).reshape(128, -1).astype(np.uint16)


def unstriped8(offs):
    return offs.reshape(8, 16, -1).transpose(0, 2, 1).reshape(8, -1).astype(np.int64)


def pick8(x, idx, run):
    r = np.arange(len(x))
    return x[r[:, None], idx[r % (8 * run) // run]]


E2M1 = np.array([0.0, 0.5, 1.0, 1.5, 2.0, 3.0, 4.0, 6.0, -0.0, -0.5, -1.0, -1.5, -2.0, -3.0, -4.0, -6.0])


def pack_weight(w, fmt):
    k, n = w.shape
    w = f64(np.asarray(w, np.float32).astype(ml_dtypes.bfloat16)).reshape(k // 32, 32, n)
    amax = np.abs(w).max(1)
    if fmt == "e4m3":
        byte = np.frexp(amax)[1] - 1 + 127 - 7
    else:
        mant, ex = np.frexp(amax / 6.0)
        byte = np.where(mant > 0.5, ex, ex - 1) + 127
    byte = np.clip(np.where(amax > 0, byte, 1), 1, 254)
    scaled = (w * np.exp2(127.0 - byte)[:, None, :]).reshape(k, n).astype(np.float32)
    by_word = np.ascontiguousarray(scaled.reshape(k // 512, 128, 4, n).transpose(0, 1, 3, 2))
    if fmt == "e4m3":
        words = by_word.astype(ml_dtypes.float8_e4m3fn).view(np.uint8)
    else:
        c = by_word.astype(ml_dtypes.float4_e2m1fn).view(np.uint8) & 0xF
        words = (c[..., 0::2] | (c[..., 1::2] << 4)).reshape(k // 512, 128, 2 * n)
    return np.ascontiguousarray(words), np.ascontiguousarray(byte.astype(np.uint8).reshape(k // 512, 16, n))


def unpack_weight(words, scales, fmt):
    g, _, n = scales.shape
    words = np.ascontiguousarray(words).reshape(g, 128, n, -1)
    if fmt == "e4m3":
        vals = words.view(ml_dtypes.float8_e4m3fn).astype(np.float64)
    else:
        nib = np.empty((g, 128, n, 4), np.uint8)
        nib[..., 0::2] = words & 0xF
        nib[..., 1::2] = words >> 4
        vals = E2M1[nib]
    vals = vals * np.repeat(np.exp2(scales.astype(np.float64) - 127.0), 8, axis=1)[..., None]
    return vals.transpose(0, 1, 3, 2).reshape(g * 512, n)


K, J, R, T, Z, M, C, O, S, N, V = 512, 512, 512, 1024, 512, 1024, 1024, 256, 256, 256, 1024


def setup_inputs():
    n = np.random.standard_normal
    idx = np.random.permutation(T)[:J]
    idx2 = np.random.permutation(M)[:J]
    idx3 = np.stack([np.random.permutation(C)[:J] for _ in range(8)])
    idx4 = np.stack([np.random.permutation(C)[:S] for _ in range(8)])
    idx5 = np.stack([np.random.permutation(C)[:S] for _ in range(8)])
    idx6 = np.stack([np.random.permutation(C)[:O] for _ in range(8)])
    idx7 = np.random.permutation(V)[:N]
    fk = mx_kscale(K)
    fr = mx_kscale(R)
    fz = mx_kscale(Z)
    xtp = pack_weight(n((K, T)) * fk[:, None], "e4m3")
    wp = pack_weight(n((K, R)) * 1 / np.sqrt(K) / fk[:, None] * fr, "e2m1")
    xop = pack_weight(n((Z, M)) / fz[:, None], "e2m1")
    w2p = pack_weight(n((Z, R)) * 1 / np.sqrt(Z) * fz[:, None] * fr, "e4m3")
    vsp = pack_weight(n((R, V)) * 1 / np.sqrt(R) / fr[:, None], "e4m3")
    return {
        "xt_words": xtp[0],
        "xt_scales": xtp[1],
        "w_words": wp[0],
        "w_scales": wp[1],
        "xo_words": xop[0],
        "xo_scales": xop[1],
        "w2_words": w2p[0],
        "w2_scales": w2p[1],
        "sa": (np.random.uniform(0.5, 1.6, (R, 1))).astype(np.float32),
        "sb": (np.random.uniform(0.5, 1.6, (R, 1))).astype(np.float32),
        "vs_words": vsp[0],
        "vs_scales": vsp[1],
        "offs": striped(idx),
        "offs2": striped(idx2),
        "offs3": striped8(idx3),
        "offs4": striped8(idx4),
        "offs5": striped8(idx5),
        "offs6": striped8(idx6),
        "offs7": striped(idx7),
    }


def reference(xt_words, xt_scales, w_words, w_scales, xo_words, xo_scales, w2_words, w2_scales, sa, sb, vs_words, vs_scales, offs, offs2, offs3, offs4, offs5, offs6, offs7):
    idx = unstriped(offs)
    idx2 = unstriped(offs2)
    idx3 = unstriped8(offs3)
    idx4 = unstriped8(offs4)
    idx5 = unstriped8(offs5)
    idx6 = unstriped8(offs6)
    idx7 = unstriped(offs7)
    xtu = unpack_weight(xt_words, xt_scales, "e4m3")
    wu = unpack_weight(w_words, w_scales, "e2m1")
    xou = unpack_weight(xo_words, xo_scales, "e2m1")
    w2u = unpack_weight(w2_words, w2_scales, "e4m3")
    vsu = unpack_weight(vs_words, vs_scales, "e4m3")
    xtidxg = xtu[:, idx]
    xoidx2g = xou[:, idx2]
    a = wu.T @ xtidxg + w2u.T @ xoidx2g
    pw = np.zeros((R, C))
    pw[np.arange(R)[:, None], idx3[np.arange(R) % 512 // 64]] = a
    h1 = pick8(pw, idx4, 64) * f64(sa)
    pv = np.zeros((R, C))
    pv[np.arange(R)[:, None], idx5[np.arange(R) % 512 // 64]] = h1
    pg = pw + pv
    hid = pick8(pg, idx6, 64) * f64(sb)
    vsidx7g = vsu[:, idx7]
    hidq = mxq(hid, 0, "e4m3")
    y = vsidx7g.T @ hidq
    return y

@@ -1,0 +1,232 @@
+from contextlib import ExitStack
+
+import concourse.mybir as mybir
+
+F32 = mybir.dt.float32
+BF16 = mybir.dt.bfloat16
+I32 = mybir.dt.int32
+U32 = mybir.dt.uint32
+U16 = mybir.dt.uint16
+U8 = mybir.dt.uint8
+FP8X4 = mybir.dt.float8_e4m3fn_x4
+FP4X4 = mybir.dt.float4_e2m1fn_x4
+COPY = mybir.ActivationFunctionType.Copy
+ADD = mybir.AluOpType.add
+
+P = 128
+PACK = 4
+SLOTS = 512
+TABLE = 1024
+BOARD = 1024
+ECHOES = 256
+PLACES = 256
+FEATURES = 256
+HIDDEN = 512
+CHUNK = 128
+CHUNKS = SLOTS // CHUNK
+HALF = PLACES // 2
+
+FLOPS = 2 * 2 * 512 * HIDDEN * SLOTS + 2 * HIDDEN * FEATURES * PLACES
+
+
+def tile_picked_tokens_plain_bank_echo_store_plain_kernel(
+    tc, xt_words, xt_scales, w_words, w_scales, xo_words, xo_scales, w2_words, w2_scales,
+    sa, sb, vs_words, vs_scales, offs, offs2, offs3, offs4, offs5, offs6, offs7, out,
+):
+    nc = tc.nc
+    with ExitStack() as ctx:
+        lists = ctx.enter_context(tc.tile_pool(name="lists", bufs=1))
+        keep = ctx.enter_context(tc.tile_pool(name="keep", bufs=1))
+        ring = ctx.enter_context(tc.tile_pool(name="ring", bufs=2))
+        psum = ctx.enter_context(tc.psum_pool(name="psum", bufs=1))
+
+        def load_list(source, name):
+            tile = lists.tile(list(source.shape), U16, name=name)
+            nc.sync.dma_start(tile[:], source)
+            return tile
+
+        def load_scale_rows_two_ports(source, name):
+            width = source.shape[2] // 4
+            stage = keep.tile([P, 2, width], I32, name=name, align_bytes=64)
+            rows = source[0].bitcast(I32).rearrange("(q j) c -> j q c", j=4)
+            for half in range(2):
+                nc.sync.dma_start(stage[64 * half : 64 * half + 4], rows[:, 2 * half : 2 * half + 2, :])
+            return lambda q: stage[64 * (q // 2) : 64 * (q // 2) + 4, q % 2, :]
+
+        def load_scale_rows(source, name):
+            width = source.shape[2] // 4
+            stage = keep.tile([4, 4, width], I32, name=name, align_bytes=64)
+            nc.sync.dma_start(stage[:], source[0].bitcast(I32).rearrange("(q j) c -> j q c", j=4))
+            return lambda q: stage[:, q, :]
+
+        def zeroed_plane(width, name, tag):
+            plane = keep.tile([P, width], U8, name=name, tag=tag, align_bytes=64)
+            nc.vector.memset(plane[:].bitcast(I32), 0)
+            return plane
+
+        def spread(pairs):
+            for q in range(4):
+                for plane, rows in pairs:
+                    nc.vector.tensor_copy(plane[:].bitcast(I32)[32 * q : 32 * q + 4, :], rows(q))
+
+        def load_words(source, dtype, name, tag):
+            width = source.shape[1] // (4 if dtype == I32 else 2)
+            tile = keep.tile([P, width], dtype, name=name, tag=tag, align_bytes=64)
+            nc.sync.dma_start(tile[:] if dtype == I32 else tile[:].bitcast(I32), source.bitcast(I32))
+            return tile
+
+        merged = "p n t -> p (n t)"
+
+        xt_rows = load_scale_rows_two_ports(xt_scales, "xt_rows")
+        xo_rows = load_scale_rows_two_ports(xo_scales, "xo_rows")
+        token_list = load_list(offs, "token_list")
+        note_list = load_list(offs2, "note_list")
+        xt_table = load_words(xt_words[0].rearrange(merged), I32, "xt_table", "xt_table")
+        xo_table = load_words(xo_words[0], U16, "xo_table", "xo_table")
+        w_rows = load_scale_rows(w_scales, "w_rows")
+        w2_rows = load_scale_rows(w2_scales, "w2_rows")
+        w2_raw = load_words(w2_words[0].rearrange(merged), I32, "w2_raw", "w2_raw")
+        w_raw = load_words(w_words[0], U16, "w_raw", "w_raw")
+        put_list = load_list(offs3, "put_list")
+        sa_cols = keep.tile([P, PACK], F32, name="sa_cols")
+        nc.sync.dma_start(sa_cols[:], sa.rearrange("(p t) o -> p (t o)", t=PACK))
+        take_list = load_list(offs4, "take_list")
+        echo_list = load_list(offs5, "echo_list")
+        read_list = load_list(offs6, "read_list")
+        store_list = load_list(offs7, "store_list")
+        sb_cols = keep.tile([P, PACK], F32, name="sb_cols")
+        nc.sync.dma_start(sb_cols[:], sb.rearrange("(p t) o -> p (t o)", t=PACK))
+        vs_rows = load_scale_rows(vs_scales, "vs_rows")
+
+        xt_plane = zeroed_plane(TABLE, "xt_plane", "xt_plane")
+        xo_plane = zeroed_plane(TABLE, "xo_plane", "xo_plane")
+        w_plane = zeroed_plane(HIDDEN, "w_plane", "w_plane")
+        w2_plane = zeroed_plane(HIDDEN, "w2_plane", "w2_plane")
+        first_boards = []
+        for b in range(2):
+            board = keep.tile([P, BOARD], F32, name=f"first_board{b}")
+            nc.vector.memset(board[:], 0.0)
+            first_boards.append(board)
+
+        def gather_chunk(c):
+            cols = slice(c * CHUNK // 16, (c + 1) * CHUNK // 16)
+            xt_c = ring.tile([P, CHUNK], U32, name=f"xt_c{c}", tag="xt_c", align_bytes=64)
+            xt_s = ring.tile([P, CHUNK], U8, name=f"xt_s{c}", tag="xt_s", align_bytes=64)
+            xo_c = ring.tile([P, CHUNK], U16, name=f"xo_c{c}", tag="xo_c", align_bytes=64)
+            xo_s = ring.tile([P, CHUNK], U8, name=f"xo_s{c}", tag="xo_s", align_bytes=64)
+            nc.vector.tensor_copy(xt_c[:], xt_table[:].bitcast(U32).indirect(token_list[:, cols]))
+            nc.vector.tensor_copy(xt_s[:], xt_plane[:].indirect(token_list[:, cols]))
+            nc.vector.tensor_copy(xo_c[:], xo_table[:].indirect(note_list[:, cols]))
+            nc.vector.tensor_copy(xo_s[:], xo_plane[:].indirect(note_list[:, cols]))
+            return xt_c, xt_s, xo_c, xo_s
+
+        spread([(xt_plane, xt_rows), (xo_plane, xo_rows)])
+        gathered = gather_chunk(0)
+        spread([(w_plane, w_rows), (w2_plane, w2_rows)])
+
+        dealt = "p (m t) -> p t m"
+        w_codes = keep.tile([P, PACK, P], U16, name="w_codes", align_bytes=64)
+        w2_codes = keep.tile([P, PACK, P], U32, name="w2_codes", align_bytes=64)
+        w_bytes = keep.tile([P, PACK, P], U8, name="w_bytes", align_bytes=64)
+        w2_bytes = keep.tile([P, PACK, P], U8, name="w2_bytes", align_bytes=64)
+        for pair in range(2):
+            ts = slice(2 * pair, 2 * pair + 2)
+            nc.scalar.copy(w2_codes[:, ts, :], w2_raw[:].bitcast(U32).rearrange(dealt, t=PACK)[:, ts, :])
+            nc.scalar.copy(w_codes[:, ts, :], w_raw[:].rearrange(dealt, t=PACK)[:, ts, :])
+            nc.vector.tensor_copy(w_bytes[:, ts, :], w_plane[:].rearrange(dealt, t=PACK)[:, ts, :])
+            nc.vector.tensor_copy(w2_bytes[:, ts, :], w2_plane[:].rearrange(dealt, t=PACK)[:, ts, :])
+
+        def hidden_product(acc, t, operands):
+            xt_c, xt_s, xo_c, xo_s = operands
+            nc.tensor.matmul_mx(out=acc, lhsT=w_codes[:, t, :].bitcast(FP4X4), lhsT_scale=w_bytes[:, t, :],
+                                rhs=xt_c[:].bitcast(FP8X4), rhs_scale=xt_s[:], start=True, stop=False)
+            nc.tensor.matmul_mx(out=acc, lhsT=w2_codes[:, t, :].bitcast(FP8X4), lhsT_scale=w2_bytes[:, t, :],
+                                rhs=xo_c[:].bitcast(FP4X4), rhs_scale=xo_s[:], start=False, stop=True)
+
+        late_banks = [psum.tile([P, SLOTS], F32, name=f"late_bank{i}") for i in range(2)]
+        for c in range(CHUNKS):
+            slots = slice(c * CHUNK, (c + 1) * CHUNK)
+            early = keep.tile([P, 2, CHUNK], F32, name=f"early{c}")
+            if c == 0:
+                banks = [psum.tile([P, CHUNK], F32, name=f"first_bank{t}", tag=f"bank{t}") for t in range(2)]
+                for t in range(2):
+                    hidden_product(banks[t][:], t, gathered)
+                    nc.scalar.copy(early[:, t, :], banks[t][:])
+            else:
+                bank = psum.tile([P, 2, CHUNK], F32, name=f"early_bank{c}")
+                for t in range(2):
+                    hidden_product(bank[:, t, :], t, gathered)
+                nc.vector.tensor_copy(early[:], bank[:])
+            for t in range(2):
+                hidden_product(late_banks[t][:, slots], 2 + t, gathered)
+            for t in range(2):
+                nc.scalar.activation(
+                    first_boards[t][:].indirect(put_list[:, c * CHUNK // 16 : (c + 1) * CHUNK // 16]),
+                    early[:, t, :], COPY)
+            if c + 1 < CHUNKS:
+                gathered = gather_chunk(c + 1)
+
+        second_boards = []
+        for b, tag in enumerate(("xt_table", "xo_plane")):
+            board = keep.tile([P, BOARD], F32, name=f"second_board{b}", tag=tag, align_bytes=64)
+            nc.vector.memset(board[:], 0.0)
+            second_boards.append(board)
+        late = []
+        for t in range(2):
+            values = keep.tile([P, SLOTS], F32, name=f"late{t}")
+            nc.vector.tensor_copy(values[:], late_banks[t][:])
+            late.append(values)
+
+        vs_table = load_words(vs_words[0].rearrange(merged), I32, "vs_table", "xo_table")
+        vs_plane = zeroed_plane(TABLE, "vs_plane", "xt_plane")
+        spread([(vs_plane, vs_rows)])
+        vs_codes = keep.tile([P, FEATURES], U32, name="vs_codes", align_bytes=64)
+        vs_bytes = keep.tile([P, FEATURES], U8, name="vs_bytes", align_bytes=64)
+        nc.vector.tensor_copy(vs_codes[:], vs_table[:].bitcast(U32).indirect(store_list[:]))
+        nc.vector.tensor_copy(vs_bytes[:], vs_plane[:].indirect(store_list[:]))
+
+        sums = []
+        for pair in range(2):
+            if pair == 1:
+                for b in range(2):
+                    nc.scalar.activation(first_boards[b][:].indirect(put_list[:]), late[b][:], COPY)
+            echoes = []
+            for b in range(2):
+                t = 2 * pair + b
+                echo = keep.tile([P, ECHOES], F32, name=f"echo{t}", tag=f"echo{t}", align_bytes=64)
+                nc.scalar.activation(echo[:], first_boards[b][:].indirect(take_list[:]), COPY,
+                                     scale=sa_cols[:, t : t + 1])
+                echoes.append(echo)
+            for b in range(2):
+                nc.scalar.activation(second_boards[b][:].indirect(echo_list[:]), echoes[b][:], COPY)
+                total = keep.tile([P, BOARD], F32, name=f"total{2 * pair + b}")
+                nc.vector.tensor_tensor(total[:], first_boards[b][:], second_boards[b][:], ADD)
+                sums.append(total)
+
+        hid = keep.tile([P, PACK, PLACES], BF16, name="hid", tag="echo3", align_bytes=64)
+        for t in range(PACK):
+            nc.scalar.activation(hid[:, t, :], sums[t][:].indirect(read_list[:]), COPY, scale=sb_cols[:, t : t + 1])
+
+        grouped = [keep.tile([P, HALF, PACK], BF16, name=f"grouped{h}", align_bytes=64) for h in range(2)]
+        hid_codes = [keep.tile([P, HALF], U32, name=f"hid_codes{h}", align_bytes=64) for h in range(2)]
+        hid_bytes = [keep.tile([P, HALF], U8, name=f"hid_bytes{h}", align_bytes=64) for h in range(2)]
+        for h in range(2):
+            nc.vector.tensor_copy(
+                grouped[h][:].rearrange("p (c i) t -> p c t i", i=4),
+                hid[:, :, h * HALF : (h + 1) * HALF].rearrange("p t (c i) -> p c t i", i=4))
+        for h in range(2):
+            nc.vector.quantize_mx(out=hid_codes[h][:].bitcast(FP8X4), scales=hid_bytes[h][:],
+                                  in_=grouped[h][:].rearrange("p o t -> p (o t)"))
+        out_banks = [psum.tile([P, PLACES], F32, name=f"out_bank{m}", tag=f"bank{m}") for m in range(2)]
+        for h in range(2):
+            for m in range(2):
+                features = slice(m * P, (m + 1) * P)
+                nc.tensor.matmul_mx(out=out_banks[m][:, h * HALF : (h + 1) * HALF],
+                                    lhsT=vs_codes[:, features].bitcast(FP8X4), lhsT_scale=vs_bytes[:, features],
+                                    rhs=hid_codes[h][:].bitcast(FP8X4), rhs_scale=hid_bytes[h][:],
+                                    start=True, stop=True)
+        results = [keep.tile([P, PLACES], F32, name=f"result{m}") for m in range(2)]
+        nc.vector.tensor_copy(results[0][:], out_banks[0][:])
+        nc.sync.dma_start(out[0:P, :], results[0][:])
+        nc.scalar.copy(results[1][:], out_banks[1][:])
+        nc.scalar.dma_start(out[P : 2 * P, :], results[1][:])

@@ -22,8 +22,7 @@ ECHOES = 256
 PLACES = 256
 FEATURES = 256
 HIDDEN = 512
-CHUNK = 128
-CHUNKS = SLOTS // CHUNK
+CHUNKS = ((0, 128), (128, 256), (256, 512))
 HALF = PLACES // 2
 
 FLOPS = 2 * 2 * 512 * HIDDEN * SLOTS + 2 * HIDDEN * FEATURES * PLACES
@@ -37,7 +36,6 @@ def tile_picked_tokens_plain_bank_echo_store_plain_kernel(
     with ExitStack() as ctx:
         lists = ctx.enter_context(tc.tile_pool(name="lists", bufs=1))
         keep = ctx.enter_context(tc.tile_pool(name="keep", bufs=1))
-        ring = ctx.enter_context(tc.tile_pool(name="ring", bufs=2))
         psum = ctx.enter_context(tc.psum_pool(name="psum", bufs=1))
 
         def load_list(source, name):
@@ -45,19 +43,20 @@ def tile_picked_tokens_plain_bank_echo_store_plain_kernel(
             nc.sync.dma_start(tile[:], source)
             return tile
 
-        def load_scale_rows_two_ports(source, name):
-            width = source.shape[2] // 4
-            stage = keep.tile([P, 2, width], I32, name=name, align_bytes=64)
-            rows = source[0].bitcast(I32).rearrange("(q j) c -> j q c", j=4)
-            for half in range(2):
-                nc.sync.dma_start(stage[64 * half : 64 * half + 4], rows[:, 2 * half : 2 * half + 2, :])
-            return lambda q: stage[64 * (q // 2) : 64 * (q // 2) + 4, q % 2, :]
-
         def load_scale_rows(source, name):
             width = source.shape[2] // 4
             stage = keep.tile([4, 4, width], I32, name=name, align_bytes=64)
             nc.sync.dma_start(stage[:], source[0].bitcast(I32).rearrange("(q j) c -> j q c", j=4))
             return lambda q: stage[:, q, :]
+
+        def load_scale_pairs(source, name):
+            width = source.shape[2] // 4
+            stage = keep.tile([64, 2, width], I32, name=name, align_bytes=64)
+            nc.vector.memset(stage[:], 0)
+            rows = source[0].bitcast(I32).rearrange("(h a j) c -> a j h c", h=2, a=2)
+            for a in range(2):
+                nc.sync.dma_start(stage[32 * a : 32 * a + 4], rows[a])
+            return stage
 
         def zeroed_plane(width, name, tag):
             plane = keep.tile([P, width], U8, name=name, tag=tag, align_bytes=64)
@@ -77,16 +76,17 @@ def tile_picked_tokens_plain_bank_echo_store_plain_kernel(
 
         merged = "p n t -> p (n t)"
 
-        xt_rows = load_scale_rows_two_ports(xt_scales, "xt_rows")
-        xo_rows = load_scale_rows_two_ports(xo_scales, "xo_rows")
+        weight_rows = keep.tile([4, 2, 4, HIDDEN // 4], I32, name="weight_rows", align_bytes=64)
+        for u, source in enumerate((w_scales, w2_scales)):
+            nc.sync.dma_start(weight_rows[:, u], source[0].bitcast(I32).rearrange("(q j) c -> j q c", j=4))
+        xt_rows = load_scale_pairs(xt_scales, "xt_rows")
+        xo_rows = load_scale_pairs(xo_scales, "xo_rows")
         token_list = load_list(offs, "token_list")
-        note_list = load_list(offs2, "note_list")
         xt_table = load_words(xt_words[0].rearrange(merged), I32, "xt_table", "xt_table")
+        note_list = load_list(offs2, "note_list")
         xo_table = load_words(xo_words[0], U16, "xo_table", "xo_table")
-        w_rows = load_scale_rows(w_scales, "w_rows")
-        w2_rows = load_scale_rows(w2_scales, "w2_rows")
-        w2_raw = load_words(w2_words[0].rearrange(merged), I32, "w2_raw", "w2_raw")
         w_raw = load_words(w_words[0], U16, "w_raw", "w_raw")
+        w2_raw = load_words(w2_words[0].rearrange(merged), I32, "w2_raw", "w2_raw")
         put_list = load_list(offs3, "put_list")
         sa_cols = keep.tile([P, PACK], F32, name="sa_cols")
         nc.sync.dma_start(sa_cols[:], sa.rearrange("(p t) o -> p (t o)", t=PACK))
@@ -98,110 +98,99 @@ def tile_picked_tokens_plain_bank_echo_store_plain_kernel(
         nc.sync.dma_start(sb_cols[:], sb.rearrange("(p t) o -> p (t o)", t=PACK))
         vs_rows = load_scale_rows(vs_scales, "vs_rows")
 
-        xt_plane = zeroed_plane(TABLE, "xt_plane", "xt_plane")
-        xo_plane = zeroed_plane(TABLE, "xo_plane", "xo_plane")
-        w_plane = zeroed_plane(HIDDEN, "w_plane", "w_plane")
-        w2_plane = zeroed_plane(HIDDEN, "w2_plane", "w2_plane")
+        weight_plane = zeroed_plane(2 * HIDDEN, "weight_plane", "weight_plane")
         first_boards = []
-        for b in range(2):
-            board = keep.tile([P, BOARD], F32, name=f"first_board{b}")
+        for t in range(PACK):
+            board = keep.tile([P, BOARD], F32, name=f"first_board{t}")
             nc.vector.memset(board[:], 0.0)
             first_boards.append(board)
 
-        def gather_chunk(c):
-            cols = slice(c * CHUNK // 16, (c + 1) * CHUNK // 16)
-            xt_c = ring.tile([P, CHUNK], U32, name=f"xt_c{c}", tag="xt_c", align_bytes=64)
-            xt_s = ring.tile([P, CHUNK], U8, name=f"xt_s{c}", tag="xt_s", align_bytes=64)
-            xo_c = ring.tile([P, CHUNK], U16, name=f"xo_c{c}", tag="xo_c", align_bytes=64)
-            xo_s = ring.tile([P, CHUNK], U8, name=f"xo_s{c}", tag="xo_s", align_bytes=64)
-            nc.vector.tensor_copy(xt_c[:], xt_table[:].bitcast(U32).indirect(token_list[:, cols]))
-            nc.vector.tensor_copy(xt_s[:], xt_plane[:].indirect(token_list[:, cols]))
-            nc.vector.tensor_copy(xo_c[:], xo_table[:].indirect(note_list[:, cols]))
-            nc.vector.tensor_copy(xo_s[:], xo_plane[:].indirect(note_list[:, cols]))
-            return xt_c, xt_s, xo_c, xo_s
-
-        spread([(xt_plane, xt_rows), (xo_plane, xo_rows)])
-        gathered = gather_chunk(0)
-        spread([(w_plane, w_rows), (w2_plane, w2_rows)])
+        xt_plane = keep.tile([P, TABLE], U8, name="xt_plane", align_bytes=64)
+        xo_plane = keep.tile([P, TABLE], U8, name="xo_plane", align_bytes=64)
+        weight_words = weight_plane[:].bitcast(I32).rearrange("p (u c) -> p u c", u=2)
+        for q in (1, 0, 2, 3):
+            nc.vector.tensor_copy(weight_words[32 * q : 32 * q + 4], weight_rows[:, :, q, :])
+            if q % 2 == 0:
+                for plane, rows in ((xt_plane, xt_rows), (xo_plane, xo_rows)):
+                    nc.vector.tensor_copy(plane[:].bitcast(I32)[32 * q : 32 * q + 64, :], rows[:, q // 2, :])
 
         dealt = "p (m t) -> p t m"
         w_codes = keep.tile([P, PACK, P], U16, name="w_codes", align_bytes=64)
         w2_codes = keep.tile([P, PACK, P], U32, name="w2_codes", align_bytes=64)
-        w_bytes = keep.tile([P, PACK, P], U8, name="w_bytes", align_bytes=64)
-        w2_bytes = keep.tile([P, PACK, P], U8, name="w2_bytes", align_bytes=64)
-        for pair in range(2):
-            ts = slice(2 * pair, 2 * pair + 2)
-            nc.scalar.copy(w2_codes[:, ts, :], w2_raw[:].bitcast(U32).rearrange(dealt, t=PACK)[:, ts, :])
-            nc.scalar.copy(w_codes[:, ts, :], w_raw[:].rearrange(dealt, t=PACK)[:, ts, :])
-            nc.vector.tensor_copy(w_bytes[:, ts, :], w_plane[:].rearrange(dealt, t=PACK)[:, ts, :])
-            nc.vector.tensor_copy(w2_bytes[:, ts, :], w2_plane[:].rearrange(dealt, t=PACK)[:, ts, :])
+        weight_bytes = keep.tile([P, PACK, 2, P], U8, name="weight_bytes", align_bytes=64)
+        nc.scalar.copy(w_codes[:], w_raw[:].rearrange(dealt, t=PACK))
+        nc.scalar.copy(w2_codes[:], w2_raw[:].bitcast(U32).rearrange(dealt, t=PACK))
+        nc.vector.tensor_copy(weight_bytes[:], weight_plane[:].rearrange("p (u m t) -> p t u m", u=2, t=PACK))
 
-        def hidden_product(acc, t, operands):
-            xt_c, xt_s, xo_c, xo_s = operands
-            nc.tensor.matmul_mx(out=acc, lhsT=w_codes[:, t, :].bitcast(FP4X4), lhsT_scale=w_bytes[:, t, :],
-                                rhs=xt_c[:].bitcast(FP8X4), rhs_scale=xt_s[:], start=True, stop=False)
-            nc.tensor.matmul_mx(out=acc, lhsT=w2_codes[:, t, :].bitcast(FP8X4), lhsT_scale=w2_bytes[:, t, :],
-                                rhs=xo_c[:].bitcast(FP4X4), rhs_scale=xo_s[:], start=False, stop=True)
+        def hidden_product(acc, t, picked):
+            xt_codes, xt_bytes, xo_codes, xo_bytes = picked
+            nc.tensor.matmul_mx(out=acc, lhsT=w_codes[:, t, :].bitcast(FP4X4), lhsT_scale=weight_bytes[:, t, 0, :],
+                                rhs=xt_codes.bitcast(FP8X4), rhs_scale=xt_bytes, start=True, stop=False)
+            nc.tensor.matmul_mx(out=acc, lhsT=w2_codes[:, t, :].bitcast(FP8X4), lhsT_scale=weight_bytes[:, t, 1, :],
+                                rhs=xo_codes.bitcast(FP4X4), rhs_scale=xo_bytes, start=False, stop=True)
 
-        late_banks = [psum.tile([P, SLOTS], F32, name=f"late_bank{i}") for i in range(2)]
-        for c in range(CHUNKS):
-            slots = slice(c * CHUNK, (c + 1) * CHUNK)
-            early = keep.tile([P, 2, CHUNK], F32, name=f"early{c}")
-            if c == 0:
-                banks = [psum.tile([P, CHUNK], F32, name=f"first_bank{t}", tag=f"bank{t}") for t in range(2)]
-                for t in range(2):
-                    hidden_product(banks[t][:], t, gathered)
-                    nc.scalar.copy(early[:, t, :], banks[t][:])
-            else:
-                bank = psum.tile([P, 2, CHUNK], F32, name=f"early_bank{c}")
-                for t in range(2):
-                    hidden_product(bank[:, t, :], t, gathered)
-                nc.vector.tensor_copy(early[:], bank[:])
-            for t in range(2):
-                hidden_product(late_banks[t][:, slots], 2 + t, gathered)
-            for t in range(2):
-                nc.scalar.activation(
-                    first_boards[t][:].indirect(put_list[:, c * CHUNK // 16 : (c + 1) * CHUNK // 16]),
-                    early[:, t, :], COPY)
-            if c + 1 < CHUNKS:
-                gathered = gather_chunk(c + 1)
+        def picked_tiles(width, label):
+            return [
+                keep.tile([P, width], dtype, name=f"{name}_{label}", tag=name, align_bytes=64)
+                for name, dtype in (("xt_codes", U32), ("xt_bytes", U8), ("xo_codes", U16), ("xo_bytes", U8))
+            ]
+
+        for c, (first, last) in enumerate(CHUNKS):
+            width = last - first
+            cols = slice(first // 16, last // 16)
+            if c < 2:
+                tiles, origin = picked_tiles(width if c == 0 else SLOTS - first, c), first
+            picked = [tile[:, first - origin : last - origin] for tile in tiles]
+            nc.vector.tensor_copy(picked[1], xt_plane[:].indirect(token_list[:, cols]))
+            nc.vector.tensor_copy(picked[3], xo_plane[:].indirect(note_list[:, cols]))
+            nc.vector.tensor_copy(picked[0], xt_table[:].bitcast(U32).indirect(token_list[:, cols]))
+            nc.vector.tensor_copy(picked[2], xo_table[:].indirect(note_list[:, cols]))
+            groups = ((0,), (1,), (2, 3)) if c < 2 else ((0, 1), (2, 3))
+            hidden = []
+            for group in groups:
+                bank = psum.tile([P, len(group), width], F32, name=f"bank{c}_{group[0]}", tag=f"bank{c}_{group[0]}")
+                for i, t in enumerate(group):
+                    hidden_product(bank[:, i, :], t, picked)
+                values = keep.tile([P, len(group), width], F32, name=f"hidden{c}_{group[0]}")
+                if len(group) == 1:
+                    nc.scalar.copy(values[:], bank[:])
+                else:
+                    nc.vector.tensor_copy(values[:], bank[:])
+                hidden.extend(values[:, i, :] for i in range(len(group)))
+            for t in range(PACK):
+                nc.scalar.activation(first_boards[t][:].indirect(put_list[:, cols]), hidden[t], COPY)
 
         second_boards = []
-        for b, tag in enumerate(("xt_table", "xo_plane")):
+        for b, tag in enumerate(("xt_codes", "xo_codes")):
             board = keep.tile([P, BOARD], F32, name=f"second_board{b}", tag=tag, align_bytes=64)
             nc.vector.memset(board[:], 0.0)
             second_boards.append(board)
-        late = []
-        for t in range(2):
-            values = keep.tile([P, SLOTS], F32, name=f"late{t}")
-            nc.vector.tensor_copy(values[:], late_banks[t][:])
-            late.append(values)
 
-        vs_table = load_words(vs_words[0].rearrange(merged), I32, "vs_table", "xo_table")
-        vs_plane = zeroed_plane(TABLE, "vs_plane", "xt_plane")
+        vs_table = load_words(vs_words[0].rearrange(merged), I32, "vs_table", "xt_table")
+        vs_plane = zeroed_plane(TABLE, "vs_plane", "xt_bytes")
         spread([(vs_plane, vs_rows)])
         vs_codes = keep.tile([P, FEATURES], U32, name="vs_codes", align_bytes=64)
         vs_bytes = keep.tile([P, FEATURES], U8, name="vs_bytes", align_bytes=64)
         nc.vector.tensor_copy(vs_codes[:], vs_table[:].bitcast(U32).indirect(store_list[:]))
         nc.vector.tensor_copy(vs_bytes[:], vs_plane[:].indirect(store_list[:]))
 
+        echoes = []
+
+        def take(t):
+            echo = keep.tile([P, ECHOES], F32, name=f"echo{t}", tag=f"echo{t}", align_bytes=64)
+            nc.scalar.activation(echo[:], first_boards[t][:].indirect(take_list[:]), COPY, scale=sa_cols[:, t : t + 1])
+            echoes.append(echo)
+
         sums = []
-        for pair in range(2):
-            if pair == 1:
-                for b in range(2):
-                    nc.scalar.activation(first_boards[b][:].indirect(put_list[:]), late[b][:], COPY)
-            echoes = []
-            for b in range(2):
-                t = 2 * pair + b
-                echo = keep.tile([P, ECHOES], F32, name=f"echo{t}", tag=f"echo{t}", align_bytes=64)
-                nc.scalar.activation(echo[:], first_boards[b][:].indirect(take_list[:]), COPY,
-                                     scale=sa_cols[:, t : t + 1])
-                echoes.append(echo)
-            for b in range(2):
-                nc.scalar.activation(second_boards[b][:].indirect(echo_list[:]), echoes[b][:], COPY)
-                total = keep.tile([P, BOARD], F32, name=f"total{2 * pair + b}")
-                nc.vector.tensor_tensor(total[:], first_boards[b][:], second_boards[b][:], ADD)
-                sums.append(total)
+        take(0)
+        take(1)
+        for t in range(PACK):
+            nc.scalar.activation(second_boards[t % 2][:].indirect(echo_list[:]), echoes[t][:], COPY)
+            if t + 2 < PACK:
+                take(t + 2)
+            total = keep.tile([P, BOARD], F32, name=f"total{t}")
+            nc.vector.tensor_tensor(total[:], first_boards[t][:], second_boards[t % 2][:], ADD)
+            sums.append(total)
 
         hid = keep.tile([P, PACK, PLACES], BF16, name="hid", tag="echo3", align_bytes=64)
         for t in range(PACK):
@@ -210,23 +199,25 @@ def tile_picked_tokens_plain_bank_echo_store_plain_kernel(
         grouped = [keep.tile([P, HALF, PACK], BF16, name=f"grouped{h}", align_bytes=64) for h in range(2)]
         hid_codes = [keep.tile([P, HALF], U32, name=f"hid_codes{h}", align_bytes=64) for h in range(2)]
         hid_bytes = [keep.tile([P, HALF], U8, name=f"hid_bytes{h}", align_bytes=64) for h in range(2)]
-        for h in range(2):
-            nc.vector.tensor_copy(
-                grouped[h][:].rearrange("p (c i) t -> p c t i", i=4),
-                hid[:, :, h * HALF : (h + 1) * HALF].rearrange("p t (c i) -> p c t i", i=4))
+        for rows in (slice(0, PACK - 1), slice(PACK - 1, PACK)):
+            for h in range(2):
+                nc.vector.tensor_copy(
+                    grouped[h][:, :, rows], hid[:, rows, h * HALF : (h + 1) * HALF].rearrange("p t o -> p o t"))
         for h in range(2):
             nc.vector.quantize_mx(out=hid_codes[h][:].bitcast(FP8X4), scales=hid_bytes[h][:],
                                   in_=grouped[h][:].rearrange("p o t -> p (o t)"))
-        out_banks = [psum.tile([P, PLACES], F32, name=f"out_bank{m}", tag=f"bank{m}") for m in range(2)]
         for h in range(2):
+            places = slice(h * HALF, (h + 1) * HALF)
             for m in range(2):
                 features = slice(m * P, (m + 1) * P)
-                nc.tensor.matmul_mx(out=out_banks[m][:, h * HALF : (h + 1) * HALF],
-                                    lhsT=vs_codes[:, features].bitcast(FP8X4), lhsT_scale=vs_bytes[:, features],
+                bank = psum.tile([P, HALF], F32, name=f"out_bank{h}_{m}", tag=f"bank{h}_{m}")
+                nc.tensor.matmul_mx(out=bank[:], lhsT=vs_codes[:, features].bitcast(FP8X4), lhsT_scale=vs_bytes[:, features],
                                     rhs=hid_codes[h][:].bitcast(FP8X4), rhs_scale=hid_bytes[h][:],
                                     start=True, stop=True)
-        results = [keep.tile([P, PLACES], F32, name=f"result{m}") for m in range(2)]
-        nc.vector.tensor_copy(results[0][:], out_banks[0][:])
-        nc.sync.dma_start(out[0:P, :], results[0][:])
-        nc.scalar.copy(results[1][:], out_banks[1][:])
-        nc.scalar.dma_start(out[P : 2 * P, :], results[1][:])
+                result = keep.tile([P, HALF], F32, name=f"result{h}_{m}")
+                if h == 1 and m == 0:
+                    nc.vector.tensor_copy(result[:], bank[:])
+                else:
+                    nc.scalar.copy(result[:], bank[:])
+                queue = nc.scalar if (h, m) == (1, 1) else nc.sync
+                queue.dma_start(out[features, places], result[:])

@@ -36,6 +36,7 @@ def tile_picked_tokens_plain_bank_echo_store_plain_kernel(
     with ExitStack() as ctx:
         lists = ctx.enter_context(tc.tile_pool(name="lists", bufs=1))
         keep = ctx.enter_context(tc.tile_pool(name="keep", bufs=1))
+        shared = ctx.enter_context(tc.tile_pool(name="shared", bufs=1))
         psum = ctx.enter_context(tc.psum_pool(name="psum", bufs=1))
 
         def load_list(source, name):
@@ -81,12 +82,12 @@ def tile_picked_tokens_plain_bank_echo_store_plain_kernel(
             nc.sync.dma_start(weight_rows[:, u], source[0].bitcast(I32).rearrange("(q j) c -> j q c", j=4))
         xt_rows = load_scale_pairs(xt_scales, "xt_rows")
         xo_rows = load_scale_pairs(xo_scales, "xo_rows")
-        token_list = load_list(offs, "token_list")
-        xt_table = load_words(xt_words[0].rearrange(merged), I32, "xt_table", "xt_table")
-        note_list = load_list(offs2, "note_list")
-        xo_table = load_words(xo_words[0], U16, "xo_table", "xo_table")
-        w_raw = load_words(w_words[0], U16, "w_raw", "w_raw")
         w2_raw = load_words(w2_words[0].rearrange(merged), I32, "w2_raw", "w2_raw")
+        xt_table = load_words(xt_words[0].rearrange(merged), I32, "xt_table", "xt_table")
+        token_list = load_list(offs, "token_list")
+        note_list = load_list(offs2, "note_list")
+        w_raw = load_words(w_words[0], U16, "w_raw", "w_raw")
+        xo_table = load_words(xo_words[0], U16, "xo_table", "xo_table")
         put_list = load_list(offs3, "put_list")
         sa_cols = keep.tile([P, PACK], F32, name="sa_cols")
         nc.sync.dma_start(sa_cols[:], sa.rearrange("(p t) o -> p (t o)", t=PACK))
@@ -98,9 +99,10 @@ def tile_picked_tokens_plain_bank_echo_store_plain_kernel(
         nc.sync.dma_start(sb_cols[:], sb.rearrange("(p t) o -> p (t o)", t=PACK))
         vs_rows = load_scale_rows(vs_scales, "vs_rows")
 
-        weight_plane = zeroed_plane(2 * HIDDEN, "weight_plane", "weight_plane")
+        weight_plane = shared.tile([P, 2 * HIDDEN], U8, name="weight_plane", align_bytes=64, offset=4 * BOARD - HIDDEN)
+        nc.vector.memset(weight_plane[:].bitcast(I32), 0)
         first_boards = []
-        for t in range(PACK):
+        for t in range(2):
             board = keep.tile([P, BOARD], F32, name=f"first_board{t}")
             nc.vector.memset(board[:], 0.0)
             first_boards.append(board)
@@ -118,9 +120,14 @@ def tile_picked_tokens_plain_bank_echo_store_plain_kernel(
         w_codes = keep.tile([P, PACK, P], U16, name="w_codes", align_bytes=64)
         w2_codes = keep.tile([P, PACK, P], U32, name="w2_codes", align_bytes=64)
         weight_bytes = keep.tile([P, PACK, 2, P], U8, name="weight_bytes", align_bytes=64)
-        nc.scalar.copy(w_codes[:], w_raw[:].rearrange(dealt, t=PACK))
         nc.scalar.copy(w2_codes[:], w2_raw[:].bitcast(U32).rearrange(dealt, t=PACK))
+        nc.scalar.copy(w_codes[:], w_raw[:].rearrange(dealt, t=PACK))
         nc.vector.tensor_copy(weight_bytes[:], weight_plane[:].rearrange("p (u m t) -> p t u m", u=2, t=PACK))
+
+        for t in range(2, PACK):
+            board = shared.tile([P, BOARD], F32, name=f"first_board{t}", align_bytes=64, offset=4 * BOARD * (t - 2))
+            nc.gpsimd.memset(board[:], 0.0)
+            first_boards.append(board)
 
         def hidden_product(acc, t, picked):
             xt_codes, xt_bytes, xo_codes, xo_bytes = picked
@@ -161,13 +168,13 @@ def tile_picked_tokens_plain_bank_echo_store_plain_kernel(
                 nc.scalar.activation(first_boards[t][:].indirect(put_list[:, cols]), hidden[t], COPY)
 
         second_boards = []
-        for b, tag in enumerate(("xt_codes", "xo_codes")):
+        for b, tag in enumerate(("xt_codes", "xt_bytes", "xo_codes", "xo_bytes")):
             board = keep.tile([P, BOARD], F32, name=f"second_board{b}", tag=tag, align_bytes=64)
             nc.vector.memset(board[:], 0.0)
             second_boards.append(board)
 
         vs_table = load_words(vs_words[0].rearrange(merged), I32, "vs_table", "xt_table")
-        vs_plane = zeroed_plane(TABLE, "vs_plane", "xt_bytes")
+        vs_plane = zeroed_plane(TABLE, "vs_plane", "xo_table")
         spread([(vs_plane, vs_rows)])
         vs_codes = keep.tile([P, FEATURES], U32, name="vs_codes", align_bytes=64)
         vs_bytes = keep.tile([P, FEATURES], U8, name="vs_bytes", align_bytes=64)
@@ -175,37 +182,33 @@ def tile_picked_tokens_plain_bank_echo_store_plain_kernel(
         nc.vector.tensor_copy(vs_bytes[:], vs_plane[:].indirect(store_list[:]))
 
         echoes = []
-
-        def take(t):
-            echo = keep.tile([P, ECHOES], F32, name=f"echo{t}", tag=f"echo{t}", align_bytes=64)
+        for t in range(PACK):
+            echo = keep.tile([P, ECHOES], F32, name=f"echo{t}")
             nc.scalar.activation(echo[:], first_boards[t][:].indirect(take_list[:]), COPY, scale=sa_cols[:, t : t + 1])
             echoes.append(echo)
 
         sums = []
-        take(0)
-        take(1)
         for t in range(PACK):
-            nc.scalar.activation(second_boards[t % 2][:].indirect(echo_list[:]), echoes[t][:], COPY)
-            if t + 2 < PACK:
-                take(t + 2)
+            nc.scalar.activation(second_boards[t][:].indirect(echo_list[:]), echoes[t][:], COPY)
             total = keep.tile([P, BOARD], F32, name=f"total{t}")
-            nc.vector.tensor_tensor(total[:], first_boards[t][:], second_boards[t % 2][:], ADD)
+            nc.vector.tensor_tensor(total[:], first_boards[t][:], second_boards[t][:], ADD)
             sums.append(total)
 
-        hid = keep.tile([P, PACK, PLACES], BF16, name="hid", tag="echo3", align_bytes=64)
+        hid = keep.tile([P, PACK, PLACES], BF16, name="hid", align_bytes=64)
         for t in range(PACK):
             nc.scalar.activation(hid[:, t, :], sums[t][:].indirect(read_list[:]), COPY, scale=sb_cols[:, t : t + 1])
 
-        grouped = [keep.tile([P, HALF, PACK], BF16, name=f"grouped{h}", align_bytes=64) for h in range(2)]
+        grouped = keep.tile([P, PLACES, PACK], BF16, name="grouped", align_bytes=64)
         hid_codes = [keep.tile([P, HALF], U32, name=f"hid_codes{h}", align_bytes=64) for h in range(2)]
         hid_bytes = [keep.tile([P, HALF], U8, name=f"hid_bytes{h}", align_bytes=64) for h in range(2)]
-        for rows in (slice(0, PACK - 1), slice(PACK - 1, PACK)):
-            for h in range(2):
-                nc.vector.tensor_copy(
-                    grouped[h][:, :, rows], hid[:, rows, h * HALF : (h + 1) * HALF].rearrange("p t o -> p o t"))
+        for rows in (slice(0, 2), slice(2, 3)):
+            nc.vector.tensor_copy(grouped[:, :, rows], hid[:, rows, :].rearrange("p t o -> p o t"))
+        for h in range(2):
+            places = slice(h * HALF, (h + 1) * HALF)
+            nc.vector.tensor_copy(grouped[:, places, PACK - 1], hid[:, PACK - 1, places])
         for h in range(2):
             nc.vector.quantize_mx(out=hid_codes[h][:].bitcast(FP8X4), scales=hid_bytes[h][:],
-                                  in_=grouped[h][:].rearrange("p o t -> p (o t)"))
+                                  in_=grouped[:, h * HALF : (h + 1) * HALF, :].rearrange("p o t -> p (o t)"))
         for h in range(2):
             places = slice(h * HALF, (h + 1) * HALF)
             for m in range(2):

@@ -15,6 +15,11 @@ ADD = mybir.AluOpType.add
 
 P = 128
 PACK = 4
+QUADRANT = 32
+LIVE = 4
+STRIPE = 16
+ALIGN = 64
+CONTRACTION = 512
 SLOTS = 512
 TABLE = 1024
 BOARD = 1024
@@ -25,7 +30,7 @@ HIDDEN = 512
 CHUNKS = ((0, 128), (128, 256), (256, 512))
 HALF = PLACES // 2
 
-FLOPS = 2 * 2 * 512 * HIDDEN * SLOTS + 2 * HIDDEN * FEATURES * PLACES
+FLOPS = 2 * 2 * CONTRACTION * HIDDEN * SLOTS + 2 * HIDDEN * FEATURES * PLACES
 
 
 def tile_picked_tokens_plain_bank_echo_store_plain_kernel(
@@ -36,7 +41,7 @@ def tile_picked_tokens_plain_bank_echo_store_plain_kernel(
     with ExitStack() as ctx:
         lists = ctx.enter_context(tc.tile_pool(name="lists", bufs=1))
         keep = ctx.enter_context(tc.tile_pool(name="keep", bufs=1))
-        shared = ctx.enter_context(tc.tile_pool(name="shared", bufs=1))
+        placed = ctx.enter_context(tc.tile_pool(name="placed", bufs=1))
         psum = ctx.enter_context(tc.psum_pool(name="psum", bufs=1))
 
         def load_list(source, name):
@@ -44,147 +49,156 @@ def tile_picked_tokens_plain_bank_echo_store_plain_kernel(
             nc.sync.dma_start(tile[:], source)
             return tile
 
-        def load_scale_rows(source, name):
-            width = source.shape[2] // 4
-            stage = keep.tile([4, 4, width], I32, name=name, align_bytes=64)
-            nc.sync.dma_start(stage[:], source[0].bitcast(I32).rearrange("(q j) c -> j q c", j=4))
-            return lambda q: stage[:, q, :]
+        def load_columns(source, name):
+            tile = keep.tile([P, PACK], F32, name=name)
+            nc.sync.dma_start(tile[:], source.rearrange("(p t) o -> p (t o)", t=PACK))
+            return tile
 
-        def load_scale_pairs(source, name):
-            width = source.shape[2] // 4
-            stage = keep.tile([64, 2, width], I32, name=name, align_bytes=64)
-            nc.vector.memset(stage[:], 0)
+        def load_fp8_words(source, name):
+            tile = keep.tile([P, source.shape[2]], I32, name=name, tag=name, align_bytes=ALIGN)
+            nc.sync.dma_start(tile[:], source[0].rearrange("p n t -> p (n t)").bitcast(I32))
+            return tile
+
+        def by_quadrant(source):
+            return source[0].bitcast(I32).rearrange("(q j) c -> j q c", j=LIVE)
+
+        def load_half_planes(source, name):
+            halves = keep.tile([P // 2, 2, source.shape[2] // 4], I32, name=name, align_bytes=ALIGN)
+            nc.vector.memset(halves[:], 0)
             rows = source[0].bitcast(I32).rearrange("(h a j) c -> a j h c", h=2, a=2)
             for a in range(2):
-                nc.sync.dma_start(stage[32 * a : 32 * a + 4], rows[a])
-            return stage
+                nc.sync.dma_start(halves[QUADRANT * a : QUADRANT * a + LIVE], rows[a])
+            return halves
 
-        def zeroed_plane(width, name, tag):
-            plane = keep.tile([P, width], U8, name=name, tag=tag, align_bytes=64)
+        def cleared_plane(width, name, tag):
+            plane = keep.tile([P, width], U8, name=name, tag=tag, align_bytes=ALIGN)
             nc.vector.memset(plane[:].bitcast(I32), 0)
             return plane
 
-        def spread(pairs):
-            for q in range(4):
-                for plane, rows in pairs:
-                    nc.vector.tensor_copy(plane[:].bitcast(I32)[32 * q : 32 * q + 4, :], rows(q))
+        def cleared_board(pool, name, **place):
+            board = pool.tile([P, BOARD], F32, name=name, **place)
+            nc.vector.memset(board[:], 0.0)
+            return board
 
-        def load_words(source, dtype, name, tag):
-            width = source.shape[1] // (4 if dtype == I32 else 2)
-            tile = keep.tile([P, width], dtype, name=name, tag=tag, align_bytes=64)
-            nc.sync.dma_start(tile[:] if dtype == I32 else tile[:].bitcast(I32), source.bitcast(I32))
-            return tile
-
-        merged = "p n t -> p (n t)"
-
-        weight_rows = keep.tile([4, 2, 4, HIDDEN // 4], I32, name="weight_rows", align_bytes=64)
+        weight_rows = keep.tile([LIVE, 2, PACK, HIDDEN // 4], I32, name="weight_rows", align_bytes=ALIGN)
         for u, source in enumerate((w_scales, w2_scales)):
-            nc.sync.dma_start(weight_rows[:, u], source[0].bitcast(I32).rearrange("(q j) c -> j q c", j=4))
-        xt_rows = load_scale_pairs(xt_scales, "xt_rows")
-        xo_rows = load_scale_pairs(xo_scales, "xo_rows")
-        w2_raw = load_words(w2_words[0].rearrange(merged), I32, "w2_raw", "w2_raw")
-        xt_table = load_words(xt_words[0].rearrange(merged), I32, "xt_table", "xt_table")
+            nc.sync.dma_start(weight_rows[:, u], by_quadrant(source))
+        xt_halves = load_half_planes(xt_scales, "xt_halves")
+        xo_halves = load_half_planes(xo_scales, "xo_halves")
+        w2_raw = load_fp8_words(w2_words, "w2_raw")
+        xt_table = load_fp8_words(xt_words, "xt_table")
         token_list = load_list(offs, "token_list")
         note_list = load_list(offs2, "note_list")
-        w_raw = load_words(w_words[0], U16, "w_raw", "w_raw")
-        xo_table = load_words(xo_words[0], U16, "xo_table", "xo_table")
+        board_bytes = 4 * BOARD
+        w_raw = placed.tile([P, HIDDEN], U16, name="w_raw", align_bytes=ALIGN, offset=board_bytes - HIDDEN)
+        nc.sync.dma_start(w_raw[:].bitcast(I32), w_words[0].bitcast(I32))
+        xo_table = keep.tile([P, TABLE], U16, name="xo_table", tag="xo_table", align_bytes=ALIGN)
+        nc.sync.dma_start(xo_table[:].bitcast(I32), xo_words[0].bitcast(I32))
         put_list = load_list(offs3, "put_list")
-        sa_cols = keep.tile([P, PACK], F32, name="sa_cols")
-        nc.sync.dma_start(sa_cols[:], sa.rearrange("(p t) o -> p (t o)", t=PACK))
+        sa_columns = load_columns(sa, "sa_columns")
         take_list = load_list(offs4, "take_list")
         echo_list = load_list(offs5, "echo_list")
         read_list = load_list(offs6, "read_list")
         store_list = load_list(offs7, "store_list")
-        sb_cols = keep.tile([P, PACK], F32, name="sb_cols")
-        nc.sync.dma_start(sb_cols[:], sb.rearrange("(p t) o -> p (t o)", t=PACK))
-        vs_rows = load_scale_rows(vs_scales, "vs_rows")
+        sb_columns = load_columns(sb, "sb_columns")
+        vs_rows = keep.tile([LIVE, PACK, TABLE // 4], I32, name="vs_rows", align_bytes=ALIGN)
+        nc.sync.dma_start(vs_rows[:], by_quadrant(vs_scales))
 
-        weight_plane = shared.tile([P, 2 * HIDDEN], U8, name="weight_plane", align_bytes=64, offset=4 * BOARD - HIDDEN)
-        nc.vector.memset(weight_plane[:].bitcast(I32), 0)
-        first_boards = []
-        for t in range(2):
-            board = keep.tile([P, BOARD], F32, name=f"first_board{t}")
-            nc.vector.memset(board[:], 0.0)
-            first_boards.append(board)
+        weight_plane = cleared_plane(2 * HIDDEN, "weight_plane", "weight_plane")
+        first_boards = [cleared_board(keep, f"first_board{t}") for t in range(2)]
 
-        xt_plane = keep.tile([P, TABLE], U8, name="xt_plane", align_bytes=64)
-        xo_plane = keep.tile([P, TABLE], U8, name="xo_plane", align_bytes=64)
-        weight_words = weight_plane[:].bitcast(I32).rearrange("p (u c) -> p u c", u=2)
+        xt_plane = keep.tile([P, TABLE], U8, name="xt_plane", align_bytes=ALIGN)
+        xo_plane = keep.tile([P, TABLE], U8, name="xo_plane", align_bytes=ALIGN)
+        weight_plane_words = weight_plane[:].bitcast(I32).rearrange("p (u c) -> p u c", u=2)
         for q in (1, 0, 2, 3):
-            nc.vector.tensor_copy(weight_words[32 * q : 32 * q + 4], weight_rows[:, :, q, :])
+            start = QUADRANT * q
+            nc.vector.tensor_copy(weight_plane_words[start : start + LIVE], weight_rows[:, :, q, :])
             if q % 2 == 0:
-                for plane, rows in ((xt_plane, xt_rows), (xo_plane, xo_rows)):
-                    nc.vector.tensor_copy(plane[:].bitcast(I32)[32 * q : 32 * q + 64, :], rows[:, q // 2, :])
+                for plane, halves in ((xt_plane, xt_halves), (xo_plane, xo_halves)):
+                    nc.vector.tensor_copy(plane[:].bitcast(I32)[start : start + P // 2, :], halves[:, q // 2, :])
 
         dealt = "p (m t) -> p t m"
-        w_codes = keep.tile([P, PACK, P], U16, name="w_codes", align_bytes=64)
-        w2_codes = keep.tile([P, PACK, P], U32, name="w2_codes", align_bytes=64)
-        weight_bytes = keep.tile([P, PACK, 2, P], U8, name="weight_bytes", align_bytes=64)
+        w_codes = keep.tile([P, PACK, P], U16, name="w_codes", align_bytes=ALIGN)
+        w2_codes = keep.tile([P, PACK, P], U32, name="w2_codes", align_bytes=ALIGN)
+        weight_bytes = keep.tile([P, PACK, 2, P], U8, name="weight_bytes", align_bytes=ALIGN)
         nc.scalar.copy(w2_codes[:], w2_raw[:].bitcast(U32).rearrange(dealt, t=PACK))
-        nc.scalar.copy(w_codes[:], w_raw[:].rearrange(dealt, t=PACK))
+        for share in (slice(0, 1), slice(1, PACK)):
+            nc.scalar.copy(w_codes[:, share, :], w_raw[:].rearrange(dealt, t=PACK)[:, share, :])
         nc.vector.tensor_copy(weight_bytes[:], weight_plane[:].rearrange("p (u m t) -> p t u m", u=2, t=PACK))
 
-        for t in range(2, PACK):
-            board = shared.tile([P, BOARD], F32, name=f"first_board{t}", align_bytes=64, offset=4 * BOARD * (t - 2))
-            nc.gpsimd.memset(board[:], 0.0)
-            first_boards.append(board)
-
-        def hidden_product(acc, t, picked):
-            xt_codes, xt_bytes, xo_codes, xo_bytes = picked
-            nc.tensor.matmul_mx(out=acc, lhsT=w_codes[:, t, :].bitcast(FP4X4), lhsT_scale=weight_bytes[:, t, 0, :],
-                                rhs=xt_codes.bitcast(FP8X4), rhs_scale=xt_bytes, start=True, stop=False)
-            nc.tensor.matmul_mx(out=acc, lhsT=w2_codes[:, t, :].bitcast(FP8X4), lhsT_scale=weight_bytes[:, t, 1, :],
-                                rhs=xo_codes.bitcast(FP4X4), rhs_scale=xo_bytes, start=False, stop=True)
+        picked_sorts = (("xt_codes", U32), ("xt_bytes", U8), ("xo_codes", U16), ("xo_bytes", U8))
 
         def picked_tiles(width, label):
             return [
-                keep.tile([P, width], dtype, name=f"{name}_{label}", tag=name, align_bytes=64)
-                for name, dtype in (("xt_codes", U32), ("xt_bytes", U8), ("xo_codes", U16), ("xo_bytes", U8))
+                keep.tile([P, width], dtype, name=f"{sort}_{label}", tag=sort, align_bytes=ALIGN)
+                for sort, dtype in picked_sorts
             ]
 
+        def multiply(c, row_tiles, picked):
+            xt_codes, xt_bytes, xo_codes, xo_bytes = picked
+            label = f"bank{c}_{row_tiles[0]}"
+            bank = psum.tile([P, len(row_tiles), xt_bytes.shape[1]], F32, name=label, tag=label)
+            for i, t in enumerate(row_tiles):
+                nc.tensor.matmul_mx(
+                    out=bank[:, i, :], lhsT=w_codes[:, t, :].bitcast(FP4X4), lhsT_scale=weight_bytes[:, t, 0, :],
+                    rhs=xt_codes.bitcast(FP8X4), rhs_scale=xt_bytes, start=True, stop=False)
+                nc.tensor.matmul_mx(
+                    out=bank[:, i, :], lhsT=w2_codes[:, t, :].bitcast(FP8X4), lhsT_scale=weight_bytes[:, t, 1, :],
+                    rhs=xo_codes.bitcast(FP4X4), rhs_scale=xo_bytes, start=False, stop=True)
+            return bank
+
+        def empty(c, row_tiles, bank, copy):
+            values = keep.tile(list(bank.shape), F32, name=f"hidden{c}_{row_tiles[0]}")
+            copy(values[:], bank[:])
+            return [values[:, i, :] for i in range(len(row_tiles))]
+
+        def entries(c):
+            return slice(CHUNKS[c][0] // STRIPE, CHUNKS[c][1] // STRIPE)
+
+        def put(c, row_tiles, values):
+            for t, rows in zip(row_tiles, values):
+                nc.scalar.activation(first_boards[t][:].indirect(put_list[:, entries(c)]), rows, COPY)
+
+        last_chunk = len(CHUNKS) - 1
+        early, late = (0, 1), (2, 3)
         for c, (first, last) in enumerate(CHUNKS):
-            width = last - first
-            cols = slice(first // 16, last // 16)
             if c < 2:
-                tiles, origin = picked_tiles(width if c == 0 else SLOTS - first, c), first
+                tiles, origin = picked_tiles(last - first if c == 0 else SLOTS - first, c), first
             picked = [tile[:, first - origin : last - origin] for tile in tiles]
-            nc.vector.tensor_copy(picked[1], xt_plane[:].indirect(token_list[:, cols]))
-            nc.vector.tensor_copy(picked[3], xo_plane[:].indirect(note_list[:, cols]))
-            nc.vector.tensor_copy(picked[0], xt_table[:].bitcast(U32).indirect(token_list[:, cols]))
-            nc.vector.tensor_copy(picked[2], xo_table[:].indirect(note_list[:, cols]))
-            groups = ((0,), (1,), (2, 3)) if c < 2 else ((0, 1), (2, 3))
-            hidden = []
-            for group in groups:
-                bank = psum.tile([P, len(group), width], F32, name=f"bank{c}_{group[0]}", tag=f"bank{c}_{group[0]}")
-                for i, t in enumerate(group):
-                    hidden_product(bank[:, i, :], t, picked)
-                values = keep.tile([P, len(group), width], F32, name=f"hidden{c}_{group[0]}")
-                if len(group) == 1:
-                    nc.scalar.copy(values[:], bank[:])
-                else:
-                    nc.vector.tensor_copy(values[:], bank[:])
-                hidden.extend(values[:, i, :] for i in range(len(group)))
-            for t in range(PACK):
-                nc.scalar.activation(first_boards[t][:].indirect(put_list[:, cols]), hidden[t], COPY)
+            nc.vector.tensor_copy(picked[1], xt_plane[:].indirect(token_list[:, entries(c)]))
+            nc.vector.tensor_copy(picked[3], xo_plane[:].indirect(note_list[:, entries(c)]))
+            nc.vector.tensor_copy(picked[0], xt_table[:].bitcast(U32).indirect(token_list[:, entries(c)]))
+            nc.vector.tensor_copy(picked[2], xo_table[:].indirect(note_list[:, entries(c)]))
+            if c < last_chunk:
+                values = [empty(c, (t,), multiply(c, (t,), picked), nc.scalar.copy)[0] for t in early]
+            else:
+                values = empty(c, early, multiply(c, early, picked), nc.vector.tensor_copy)
+            values = values + empty(c, late, multiply(c, late, picked), nc.vector.tensor_copy)
+            if c == 0:
+                first_boards.extend(
+                    cleared_board(placed, f"first_board{t}", align_bytes=ALIGN, offset=board_bytes * (t - 2))
+                    for t in range(2, PACK))
+            put(c, early + late, values)
 
-        second_boards = []
-        for b, tag in enumerate(("xt_codes", "xt_bytes", "xo_codes", "xo_bytes")):
-            board = keep.tile([P, BOARD], F32, name=f"second_board{b}", tag=tag, align_bytes=64)
-            nc.vector.memset(board[:], 0.0)
-            second_boards.append(board)
-
-        vs_table = load_words(vs_words[0].rearrange(merged), I32, "vs_table", "xt_table")
-        vs_plane = zeroed_plane(TABLE, "vs_plane", "xo_table")
-        spread([(vs_plane, vs_rows)])
-        vs_codes = keep.tile([P, FEATURES], U32, name="vs_codes", align_bytes=64)
-        vs_bytes = keep.tile([P, FEATURES], U8, name="vs_bytes", align_bytes=64)
+        second_boards = [
+            cleared_board(keep, f"second_board{t}", tag=sort, align_bytes=ALIGN)
+            for t, (sort, dtype) in enumerate(picked_sorts)
+        ]
+        vs_table = keep.tile([P, TABLE], I32, name="vs_table", tag="xt_table", align_bytes=ALIGN)
+        nc.sync.dma_start(vs_table[:], vs_words[0].rearrange("p n t -> p (n t)").bitcast(I32))
+        vs_plane = cleared_plane(TABLE, "vs_plane", "xo_table")
+        for q in range(PACK):
+            nc.vector.tensor_copy(vs_plane[:].bitcast(I32)[QUADRANT * q : QUADRANT * q + LIVE, :], vs_rows[:, q, :])
+        vs_codes = keep.tile([P, FEATURES], U32, name="vs_codes", align_bytes=ALIGN)
+        vs_bytes = keep.tile([P, FEATURES], U8, name="vs_bytes", align_bytes=ALIGN)
         nc.vector.tensor_copy(vs_codes[:], vs_table[:].bitcast(U32).indirect(store_list[:]))
         nc.vector.tensor_copy(vs_bytes[:], vs_plane[:].indirect(store_list[:]))
 
         echoes = []
         for t in range(PACK):
             echo = keep.tile([P, ECHOES], F32, name=f"echo{t}")
-            nc.scalar.activation(echo[:], first_boards[t][:].indirect(take_list[:]), COPY, scale=sa_cols[:, t : t + 1])
+            nc.scalar.activation(
+                echo[:], first_boards[t][:].indirect(take_list[:]), COPY, scale=sa_columns[:, t : t + 1])
             echoes.append(echo)
 
         sums = []
@@ -194,33 +208,33 @@ def tile_picked_tokens_plain_bank_echo_store_plain_kernel(
             nc.vector.tensor_tensor(total[:], first_boards[t][:], second_boards[t][:], ADD)
             sums.append(total)
 
-        hid = keep.tile([P, PACK, PLACES], BF16, name="hid", align_bytes=64)
+        hid = keep.tile([P, PACK, PLACES], BF16, name="hid", align_bytes=ALIGN)
         for t in range(PACK):
-            nc.scalar.activation(hid[:, t, :], sums[t][:].indirect(read_list[:]), COPY, scale=sb_cols[:, t : t + 1])
+            nc.scalar.activation(
+                hid[:, t, :], sums[t][:].indirect(read_list[:]), COPY, scale=sb_columns[:, t : t + 1])
 
-        grouped = keep.tile([P, PLACES, PACK], BF16, name="grouped", align_bytes=64)
-        hid_codes = [keep.tile([P, HALF], U32, name=f"hid_codes{h}", align_bytes=64) for h in range(2)]
-        hid_bytes = [keep.tile([P, HALF], U8, name=f"hid_bytes{h}", align_bytes=64) for h in range(2)]
-        for rows in (slice(0, 2), slice(2, 3)):
-            nc.vector.tensor_copy(grouped[:, :, rows], hid[:, rows, :].rearrange("p t o -> p o t"))
-        for h in range(2):
-            places = slice(h * HALF, (h + 1) * HALF)
+        halves_of_places = [slice(h * HALF, (h + 1) * HALF) for h in range(2)]
+        grouped = keep.tile([P, PLACES, PACK], BF16, name="grouped", align_bytes=ALIGN)
+        hid_codes = [keep.tile([P, HALF], U32, name=f"hid_codes{h}", align_bytes=ALIGN) for h in range(2)]
+        hid_bytes = [keep.tile([P, HALF], U8, name=f"hid_bytes{h}", align_bytes=ALIGN) for h in range(2)]
+        for share in (slice(0, 2), slice(2, 3)):
+            nc.vector.tensor_copy(grouped[:, :, share], hid[:, share, :].rearrange("p t o -> p o t"))
+        for places in halves_of_places:
             nc.vector.tensor_copy(grouped[:, places, PACK - 1], hid[:, PACK - 1, places])
-        for h in range(2):
-            nc.vector.quantize_mx(out=hid_codes[h][:].bitcast(FP8X4), scales=hid_bytes[h][:],
-                                  in_=grouped[:, h * HALF : (h + 1) * HALF, :].rearrange("p o t -> p (o t)"))
-        for h in range(2):
-            places = slice(h * HALF, (h + 1) * HALF)
-            for m in range(2):
+        for h, places in enumerate(halves_of_places):
+            nc.vector.quantize_mx(
+                out=hid_codes[h][:].bitcast(FP8X4), scales=hid_bytes[h][:],
+                in_=grouped[:, places, :].rearrange("p o t -> p (o t)"))
+
+        for h, places in enumerate(halves_of_places):
+            for m in range(FEATURES // P):
                 features = slice(m * P, (m + 1) * P)
                 bank = psum.tile([P, HALF], F32, name=f"out_bank{h}_{m}", tag=f"bank{h}_{m}")
-                nc.tensor.matmul_mx(out=bank[:], lhsT=vs_codes[:, features].bitcast(FP8X4), lhsT_scale=vs_bytes[:, features],
-                                    rhs=hid_codes[h][:].bitcast(FP8X4), rhs_scale=hid_bytes[h][:],
-                                    start=True, stop=True)
+                nc.tensor.matmul_mx(
+                    out=bank[:], lhsT=vs_codes[:, features].bitcast(FP8X4), lhsT_scale=vs_bytes[:, features],
+                    rhs=hid_codes[h][:].bitcast(FP8X4), rhs_scale=hid_bytes[h][:], start=True, stop=True)
                 result = keep.tile([P, HALF], F32, name=f"result{h}_{m}")
-                if h == 1 and m == 0:
-                    nc.vector.tensor_copy(result[:], bank[:])
-                else:
-                    nc.scalar.copy(result[:], bank[:])
+                copy = nc.vector.tensor_copy if (h, m) == (1, 0) else nc.scalar.copy
+                copy(result[:], bank[:])
                 queue = nc.scalar if (h, m) == (1, 1) else nc.sync
                 queue.dma_start(out[features, places], result[:])

from contextlib import ExitStack

import concourse.mybir as mybir

F32 = mybir.dt.float32
BF16 = mybir.dt.bfloat16
I32 = mybir.dt.int32
U32 = mybir.dt.uint32
U16 = mybir.dt.uint16
U8 = mybir.dt.uint8
FP8X4 = mybir.dt.float8_e4m3fn_x4
FP4X4 = mybir.dt.float4_e2m1fn_x4
COPY = mybir.ActivationFunctionType.Copy
ADD = mybir.AluOpType.add

P = 128
PACK = 4
QUADRANT = 32
LIVE = 4
STRIPE = 16
ALIGN = 64
CONTRACTION = 512
SLOTS = 512
TABLE = 1024
BOARD = 1024
ECHOES = 256
PLACES = 256
FEATURES = 256
HIDDEN = 512
CHUNKS = ((0, 128), (128, 256), (256, 512))
HALF = PLACES // 2

FLOPS = 2 * 2 * CONTRACTION * HIDDEN * SLOTS + 2 * HIDDEN * FEATURES * PLACES


def tile_picked_tokens_plain_bank_echo_store_plain_kernel(
    tc, xt_words, xt_scales, w_words, w_scales, xo_words, xo_scales, w2_words, w2_scales,
    sa, sb, vs_words, vs_scales, offs, offs2, offs3, offs4, offs5, offs6, offs7, out,
):
    nc = tc.nc
    with ExitStack() as ctx:
        lists = ctx.enter_context(tc.tile_pool(name="lists", bufs=1))
        keep = ctx.enter_context(tc.tile_pool(name="keep", bufs=1))
        placed = ctx.enter_context(tc.tile_pool(name="placed", bufs=1))
        psum = ctx.enter_context(tc.psum_pool(name="psum", bufs=1))

        def load_list(source, name):
            tile = lists.tile(list(source.shape), U16, name=name)
            nc.sync.dma_start(tile[:], source)
            return tile

        def load_columns(source, name):
            tile = keep.tile([P, PACK], F32, name=name)
            nc.sync.dma_start(tile[:], source.rearrange("(p t) o -> p (t o)", t=PACK))
            return tile

        def load_fp8_words(source, name):
            tile = keep.tile([P, source.shape[2]], I32, name=name, tag=name, align_bytes=ALIGN)
            nc.sync.dma_start(tile[:], source[0].rearrange("p n t -> p (n t)").bitcast(I32))
            return tile

        def by_quadrant(source):
            return source[0].bitcast(I32).rearrange("(q j) c -> j q c", j=LIVE)

        def load_half_planes(source, name):
            halves = keep.tile([P // 2, 2, source.shape[2] // 4], I32, name=name, align_bytes=ALIGN)
            nc.vector.memset(halves[:], 0)
            rows = source[0].bitcast(I32).rearrange("(h a j) c -> a j h c", h=2, a=2)
            for a in range(2):
                nc.sync.dma_start(halves[QUADRANT * a : QUADRANT * a + LIVE], rows[a])
            return halves

        def cleared_plane(width, name, tag):
            plane = keep.tile([P, width], U8, name=name, tag=tag, align_bytes=ALIGN)
            nc.vector.memset(plane[:].bitcast(I32), 0)
            return plane

        def cleared_board(pool, name, **place):
            board = pool.tile([P, BOARD], F32, name=name, **place)
            nc.vector.memset(board[:], 0.0)
            return board

        weight_rows = keep.tile([LIVE, 2, PACK, HIDDEN // 4], I32, name="weight_rows", align_bytes=ALIGN)
        for u, source in enumerate((w_scales, w2_scales)):
            nc.sync.dma_start(weight_rows[:, u], by_quadrant(source))
        xt_halves = load_half_planes(xt_scales, "xt_halves")
        xo_halves = load_half_planes(xo_scales, "xo_halves")
        w2_raw = load_fp8_words(w2_words, "w2_raw")
        xt_table = load_fp8_words(xt_words, "xt_table")
        token_list = load_list(offs, "token_list")
        note_list = load_list(offs2, "note_list")
        board_bytes = 4 * BOARD
        w_raw = placed.tile([P, HIDDEN], U16, name="w_raw", align_bytes=ALIGN, offset=board_bytes - HIDDEN)
        nc.sync.dma_start(w_raw[:].bitcast(I32), w_words[0].bitcast(I32))
        xo_table = keep.tile([P, TABLE], U16, name="xo_table", tag="xo_table", align_bytes=ALIGN)
        nc.sync.dma_start(xo_table[:].bitcast(I32), xo_words[0].bitcast(I32))
        put_list = load_list(offs3, "put_list")
        sa_columns = load_columns(sa, "sa_columns")
        take_list = load_list(offs4, "take_list")
        echo_list = load_list(offs5, "echo_list")
        read_list = load_list(offs6, "read_list")
        store_list = load_list(offs7, "store_list")
        sb_columns = load_columns(sb, "sb_columns")
        vs_rows = keep.tile([LIVE, PACK, TABLE // 4], I32, name="vs_rows", align_bytes=ALIGN)
        nc.sync.dma_start(vs_rows[:], by_quadrant(vs_scales))

        weight_plane = cleared_plane(2 * HIDDEN, "weight_plane", "weight_plane")
        first_boards = [cleared_board(keep, f"first_board{t}") for t in range(2)]

        xt_plane = keep.tile([P, TABLE], U8, name="xt_plane", align_bytes=ALIGN)
        xo_plane = keep.tile([P, TABLE], U8, name="xo_plane", align_bytes=ALIGN)
        weight_plane_words = weight_plane[:].bitcast(I32).rearrange("p (u c) -> p u c", u=2)
        for q in (1, 0, 2, 3):
            start = QUADRANT * q
            nc.vector.tensor_copy(weight_plane_words[start : start + LIVE], weight_rows[:, :, q, :])
            if q % 2 == 0:
                for plane, halves in ((xt_plane, xt_halves), (xo_plane, xo_halves)):
                    nc.vector.tensor_copy(plane[:].bitcast(I32)[start : start + P // 2, :], halves[:, q // 2, :])

        dealt = "p (m t) -> p t m"
        w_codes = keep.tile([P, PACK, P], U16, name="w_codes", align_bytes=ALIGN)
        w2_codes = keep.tile([P, PACK, P], U32, name="w2_codes", align_bytes=ALIGN)
        weight_bytes = keep.tile([P, PACK, 2, P], U8, name="weight_bytes", align_bytes=ALIGN)
        nc.scalar.copy(w2_codes[:], w2_raw[:].bitcast(U32).rearrange(dealt, t=PACK))
        for share in (slice(0, 1), slice(1, PACK)):
            nc.scalar.copy(w_codes[:, share, :], w_raw[:].rearrange(dealt, t=PACK)[:, share, :])
        nc.vector.tensor_copy(weight_bytes[:], weight_plane[:].rearrange("p (u m t) -> p t u m", u=2, t=PACK))

        picked_sorts = (("xt_codes", U32), ("xt_bytes", U8), ("xo_codes", U16), ("xo_bytes", U8))

        def picked_tiles(width, label):
            return [
                keep.tile([P, width], dtype, name=f"{sort}_{label}", tag=sort, align_bytes=ALIGN)
                for sort, dtype in picked_sorts
            ]

        def multiply(c, row_tiles, picked):
            xt_codes, xt_bytes, xo_codes, xo_bytes = picked
            label = f"bank{c}_{row_tiles[0]}"
            bank = psum.tile([P, len(row_tiles), xt_bytes.shape[1]], F32, name=label, tag=label)
            for i, t in enumerate(row_tiles):
                nc.tensor.matmul_mx(
                    out=bank[:, i, :], lhsT=w_codes[:, t, :].bitcast(FP4X4), lhsT_scale=weight_bytes[:, t, 0, :],
                    rhs=xt_codes.bitcast(FP8X4), rhs_scale=xt_bytes, start=True, stop=False)
                nc.tensor.matmul_mx(
                    out=bank[:, i, :], lhsT=w2_codes[:, t, :].bitcast(FP8X4), lhsT_scale=weight_bytes[:, t, 1, :],
                    rhs=xo_codes.bitcast(FP4X4), rhs_scale=xo_bytes, start=False, stop=True)
            return bank

        def empty(c, row_tiles, bank, copy):
            values = keep.tile(list(bank.shape), F32, name=f"hidden{c}_{row_tiles[0]}")
            copy(values[:], bank[:])
            return [values[:, i, :] for i in range(len(row_tiles))]

        def entries(c):
            return slice(CHUNKS[c][0] // STRIPE, CHUNKS[c][1] // STRIPE)

        def put(c, row_tiles, values):
            for t, rows in zip(row_tiles, values):
                nc.scalar.activation(first_boards[t][:].indirect(put_list[:, entries(c)]), rows, COPY)

        last_chunk = len(CHUNKS) - 1
        early, late = (0, 1), (2, 3)
        for c, (first, last) in enumerate(CHUNKS):
            if c < 2:
                tiles, origin = picked_tiles(last - first if c == 0 else SLOTS - first, c), first
            picked = [tile[:, first - origin : last - origin] for tile in tiles]
            nc.vector.tensor_copy(picked[1], xt_plane[:].indirect(token_list[:, entries(c)]))
            nc.vector.tensor_copy(picked[3], xo_plane[:].indirect(note_list[:, entries(c)]))
            nc.vector.tensor_copy(picked[0], xt_table[:].bitcast(U32).indirect(token_list[:, entries(c)]))
            nc.vector.tensor_copy(picked[2], xo_table[:].indirect(note_list[:, entries(c)]))
            if c < last_chunk:
                values = [empty(c, (t,), multiply(c, (t,), picked), nc.scalar.copy)[0] for t in early]
            else:
                values = empty(c, early, multiply(c, early, picked), nc.vector.tensor_copy)
            values = values + empty(c, late, multiply(c, late, picked), nc.vector.tensor_copy)
            if c == 0:
                first_boards.extend(
                    cleared_board(placed, f"first_board{t}", align_bytes=ALIGN, offset=board_bytes * (t - 2))
                    for t in range(2, PACK))
            put(c, early + late, values)

        second_boards = [
            cleared_board(keep, f"second_board{t}", tag=sort, align_bytes=ALIGN)
            for t, (sort, dtype) in enumerate(picked_sorts)
        ]
        vs_table = keep.tile([P, TABLE], I32, name="vs_table", tag="xt_table", align_bytes=ALIGN)
        nc.sync.dma_start(vs_table[:], vs_words[0].rearrange("p n t -> p (n t)").bitcast(I32))
        vs_plane = cleared_plane(TABLE, "vs_plane", "xo_table")
        for q in range(PACK):
            nc.vector.tensor_copy(vs_plane[:].bitcast(I32)[QUADRANT * q : QUADRANT * q + LIVE, :], vs_rows[:, q, :])
        vs_codes = keep.tile([P, FEATURES], U32, name="vs_codes", align_bytes=ALIGN)
        vs_bytes = keep.tile([P, FEATURES], U8, name="vs_bytes", align_bytes=ALIGN)
        nc.vector.tensor_copy(vs_codes[:], vs_table[:].bitcast(U32).indirect(store_list[:]))
        nc.vector.tensor_copy(vs_bytes[:], vs_plane[:].indirect(store_list[:]))

        echoes = []
        for t in range(PACK):
            echo = keep.tile([P, ECHOES], F32, name=f"echo{t}")
            nc.scalar.activation(
                echo[:], first_boards[t][:].indirect(take_list[:]), COPY, scale=sa_columns[:, t : t + 1])
            echoes.append(echo)

        sums = []
        for t in range(PACK):
            nc.scalar.activation(second_boards[t][:].indirect(echo_list[:]), echoes[t][:], COPY)
            total = keep.tile([P, BOARD], F32, name=f"total{t}")
            nc.vector.tensor_tensor(total[:], first_boards[t][:], second_boards[t][:], ADD)
            sums.append(total)

        hid = keep.tile([P, PACK, PLACES], BF16, name="hid", align_bytes=ALIGN)
        for t in range(PACK):
            nc.scalar.activation(
                hid[:, t, :], sums[t][:].indirect(read_list[:]), COPY, scale=sb_columns[:, t : t + 1])

        halves_of_places = [slice(h * HALF, (h + 1) * HALF) for h in range(2)]
        grouped = keep.tile([P, PLACES, PACK], BF16, name="grouped", align_bytes=ALIGN)
        hid_codes = [keep.tile([P, HALF], U32, name=f"hid_codes{h}", align_bytes=ALIGN) for h in range(2)]
        hid_bytes = [keep.tile([P, HALF], U8, name=f"hid_bytes{h}", align_bytes=ALIGN) for h in range(2)]
        for share in (slice(0, 2), slice(2, 3)):
            nc.vector.tensor_copy(grouped[:, :, share], hid[:, share, :].rearrange("p t o -> p o t"))
        for places in halves_of_places:
            nc.vector.tensor_copy(grouped[:, places, PACK - 1], hid[:, PACK - 1, places])
        for h, places in enumerate(halves_of_places):
            nc.vector.quantize_mx(
                out=hid_codes[h][:].bitcast(FP8X4), scales=hid_bytes[h][:],
                in_=grouped[:, places, :].rearrange("p o t -> p (o t)"))

        for h, places in enumerate(halves_of_places):
            for m in range(FEATURES // P):
                features = slice(m * P, (m + 1) * P)
                bank = psum.tile([P, HALF], F32, name=f"out_bank{h}_{m}", tag=f"bank{h}_{m}")
                nc.tensor.matmul_mx(
                    out=bank[:], lhsT=vs_codes[:, features].bitcast(FP8X4), lhsT_scale=vs_bytes[:, features],
                    rhs=hid_codes[h][:].bitcast(FP8X4), rhs_scale=hid_bytes[h][:], start=True, stop=True)
                result = keep.tile([P, HALF], F32, name=f"result{h}_{m}")
                copy = nc.vector.tensor_copy if (h, m) == (1, 0) else nc.scalar.copy
                copy(result[:], bank[:])
                queue = nc.scalar if (h, m) == (1, 1) else nc.sync
                queue.dma_start(out[features, places], result[:])
